import numpy as np
import ml_dtypes


def mxq(x, axis, fmt="e4m3"):
    dtype, down = {"e4m3": (ml_dtypes.float8_e4m3fn, 7), "e5m2": (ml_dtypes.float8_e5m2, 14)}[fmt]
    v = np.moveaxis(np.asarray(x, np.float32).astype(ml_dtypes.bfloat16).astype(np.float64), axis, -1)
    blocks = v.reshape(v.shape[:-1] + (-1, 32))
    amax = np.abs(blocks).max(-1, keepdims=True)
    byte = np.maximum(np.where(amax > 0, np.frexp(amax)[1] - 1 + 127, 0) - down, 1)
    scale = np.exp2(byte - 127.0)
    codes = (blocks / scale).astype(np.float32).astype(dtype).astype(np.float64)
    return np.moveaxis((codes * scale).reshape(v.shape), -1, axis)


WIDE = False


def mx_kscale(k):
    if not WIDE:
        return np.ones(k)
    levels = np.array([30, -30])
    if k % 512:
        return np.exp2(np.random.permutation(np.resize(levels, k // 32))).repeat(32)
    a = np.empty((k // 512, 16))
    for p in range(k // 512):
        a[p, :8] = np.random.permutation(np.resize(levels, 8))
        for g in range(8):
            far = levels[np.abs(levels - a[p, g]) >= 10]
            a[p, g + 8] = far[np.random.randint(len(far))]
    return np.exp2(a.ravel()).repeat(32)


def f64(x):
    return np.asarray(x).astype(np.float64)


def striped(idx):
    return np.tile(np.asarray(idx).reshape(-1, 16).T, (8, 1)).astype(np.uint16)


def unstriped(offs):
    return offs[:16].T.reshape(-1).astype(np.int64)


def striped8(idx):
    return np.asarray(idx).reshape(8, -1, 16).transpose(0, 2, 1).reshape(128, -1).astype(np.uint16)


def unstriped8(offs):
    return offs.reshape(8, 16, -1).transpose(0, 2, 1).reshape(8, -1).astype(np.int64)


def pick8(x, idx, run):
    r = np.arange(len(x))
    return x[r[:, None], idx[r % (8 * run) // run]]


E2M1 = np.array([0.0, 0.5, 1.0, 1.5, 2.0, 3.0, 4.0, 6.0, -0.0, -0.5, -1.0, -1.5, -2.0, -3.0, -4.0, -6.0])


def pack_weight(w, fmt):
    k, n = w.shape
    w = f64(np.asarray(w, np.float32).astype(ml_dtypes.bfloat16)).reshape(k // 32, 32, n)
    amax = np.abs(w).max(1)
    if fmt == "e4m3":
        byte = np.frexp(amax)[1] - 1 + 127 - 7
    else:
        mant, ex = np.frexp(amax / 6.0)
        byte = np.where(mant > 0.5, ex, ex - 1) + 127
    byte = np.clip(np.where(amax > 0, byte, 1), 1, 254)
    scaled = (w * np.exp2(127.0 - byte)[:, None, :]).reshape(k, n).astype(np.float32)
    by_word = np.ascontiguousarray(scaled.reshape(k // 512, 128, 4, n).transpose(0, 1, 3, 2))
    if fmt == "e4m3":
        words = by_word.astype(ml_dtypes.float8_e4m3fn).view(np.uint8)
    else:
        c = by_word.astype(ml_dtypes.float4_e2m1fn).view(np.uint8) & 0xF
        words = (c[..., 0::2] | (c[..., 1::2] << 4)).reshape(k // 512, 128, 2 * n)
    return np.ascontiguousarray(words), np.ascontiguousarray(byte.astype(np.uint8).reshape(k // 512, 16, n))


def unpack_weight(words, scales, fmt):
    g, _, n = scales.shape
    words = np.ascontiguousarray(words).reshape(g, 128, n, -1)
    if fmt == "e4m3":
        vals = words.view(ml_dtypes.float8_e4m3fn).astype(np.float64)
    else:
        nib = np.empty((g, 128, n, 4), np.uint8)
        nib[..., 0::2] = words & 0xF
        nib[..., 1::2] = words >> 4
        vals = E2M1[nib]
    vals = vals * np.repeat(np.exp2(scales.astype(np.float64) - 127.0), 8, axis=1)[..., None]
    return vals.transpose(0, 1, 3, 2).reshape(g * 512, n)


def bf(x):
    return np.asarray(x, np.float32).astype(ml_dtypes.bfloat16)


def planes(Y):
    r, m = Y.shape
    b = f64(bf(Y)).reshape(r // 32, 32, m)
    amax = np.abs(b).max(1)
    byte = np.clip(np.where(amax > 0, np.frexp(amax)[1] - 1 + 127 - 7, 1), 1, 254)
    codes = (b * np.exp2(127.0 - byte)[:, None, :]).reshape(r, m).astype(np.float32).astype(ml_dtypes.float8_e4m3fn).view(np.uint8)
    words = codes.reshape(r // 512, 128, 4, m).transpose(0, 1, 3, 2)
    return np.ascontiguousarray(words), np.ascontiguousarray(byte.astype(np.uint8).reshape(r // 512, 16, m))


N, K, T, J, V = 512, 512, 1024, 512, 1024


def setup_inputs():
    n = np.random.standard_normal
    idx = np.stack([np.random.permutation(T)[:J] for _ in range(8)])
    idx2 = np.random.permutation(V)[:J]
    fn = mx_kscale(N)
    wp = pack_weight(n((N, K)) * 1 / np.sqrt(N) * fn[:, None], "e4m3")
    return {
        "g": (n((N, T)) * np.exp(0.5 * n((1, T))) / fn[:, None]).astype(np.float32),
        "tb": (n((N, V))).astype(np.float32),
        "w_words": wp[0],
        "w_scales": wp[1],
        "rw": (np.random.uniform(0.5, 2.0, (1, J))).astype(np.float32),
        "offs": striped8(idx),
        "offs2": striped(idx2),
    }


def reference(g, tb, w_words, w_scales, rw, offs, offs2):
    idx = unstriped8(offs)
    idx2 = unstriped(offs2)
    wu = unpack_weight(w_words, w_scales, "e4m3")
    d = pick8(f64(g), idx, 64) * f64(tb)[:, idx2]
    dq = mxq(d, 0, "e5m2")
    p = wu.T @ dq
    y = p * f64(rw)
    words, scales = planes(y)
    return y, words, scales

@@ -1,0 +1,145 @@
+from contextlib import ExitStack
+
+import concourse.mybir as mybir
+from concourse.masks import make_identity
+
+N, K, T, J, V = 512, 512, 1024, 512, 1024
+FLOPS = 2 * N * K * J
+
+F32 = mybir.dt.float32
+BF16 = mybir.dt.bfloat16
+I32 = mybir.dt.int32
+U32 = mybir.dt.uint32
+U16 = mybir.dt.uint16
+U8 = mybir.dt.uint8
+E4M3 = mybir.dt.float8_e4m3fn_x4
+E5M2 = mybir.dt.float8_e5m2_x4
+COPY = mybir.ActivationFunctionType.Copy
+MULT = mybir.AluOpType.mult
+
+P = 128
+PACK = 4
+CH = 128
+NCH = J // CH
+LC = CH // 16
+
+
+def tile_moe_expert_head_gradients_by_table_pl_kernel(tc, g, tb, w_words, w_scales, rw, offs, offs2, out_0, out_1, out_2):
+    nc = tc.nc
+    with ExitStack() as ctx:
+        keep = ctx.enter_context(tc.tile_pool(name="keep", bufs=1))
+        psum = ctx.enter_context(tc.psum_pool(name="psum", bufs=1))
+
+        g_list = keep.tile([P, J // 16], U16, name="g_list")
+        tb_list = keep.tile([P, J // 16], U16, name="tb_list")
+        g_rows = g.rearrange("(p t) c -> p t c", t=PACK)
+        tb_rows = tb.rearrange("(p t) c -> p t c", t=PACK)
+        g_sb = [keep.tile([P, T], F32, name="g_sb%d" % t) for t in range(PACK)]
+        tb_sb = [keep.tile([P, V], F32, name="tb_sb%d" % t) for t in range(PACK)]
+
+        nc.sync.dma_start(tb_list[:], offs2)
+        nc.sync.dma_start(tb_sb[0][:], tb_rows[:, 0, :])
+        nc.sync.dma_start(g_list[:], offs)
+        nc.sync.dma_start(g_sb[0][:], g_rows[:, 0, :])
+        for t in range(1, PACK):
+            nc.sync.dma_start(tb_sb[t][:], tb_rows[:, t, :])
+            nc.sync.dma_start(g_sb[t][:], g_rows[:, t, :])
+
+        w_raw = keep.tile([P, K], I32, name="w_raw")
+        w_codes = keep.tile([P, PACK, P], I32, name="w_codes", align_bytes=64)
+        sc_raw = keep.tile([P, K], U8, name="sc_raw")
+        w_sc = keep.tile([P, PACK, P], U8, name="w_sc", align_bytes=64)
+        rw_col = keep.tile([P, PACK], F32, name="rw_col")
+        nc.vector.memset(sc_raw[:].bitcast(I32), 0)
+        for q in range(4):
+            nc.scalar.dma_start(sc_raw[32 * q : 32 * q + 4, :].bitcast(I32), w_scales[0, 4 * q : 4 * q + 4, :].bitcast(I32))
+        nc.sync.dma_start(w_raw[:], w_words[0].rearrange("p n t -> p (n t)").bitcast(I32))
+        nc.sync.dma_start(rw_col[:], rw.rearrange("o (p c) -> p (o c)", c=PACK))
+        nc.vector.tensor_copy(
+            w_sc[:].rearrange("p t (c i) -> p c t i", i=16), sc_raw[:].rearrange("p (c i t) -> p c t i", i=16, t=PACK)
+        )
+
+        ident = keep.tile([P, P], F32, name="ident")
+        make_identity(nc, ident[:])
+        rw_bank = psum.tile([P, PACK, P], F32, name="rw_bank")
+        for c in range(PACK):
+            nc.tensor.transpose(rw_bank[:, c, :], rw_col[:, c : c + 1].to_broadcast([P, P]), ident[:])
+        rw_all = keep.tile([P, J], F32, name="rw_all")
+        nc.scalar.copy(rw_all[:].rearrange("p (n c) -> p n c", c=PACK), rw_bank[:].rearrange("p c n -> p n c"))
+
+        tb_got = [keep.tile([P, J], F32, name="tb_got%d" % t) for t in range(PACK)]
+        d_pair = [keep.tile([P, 2, J], F32, name="d_pair%d" % u) for u in range(2)]
+        d_bf = [keep.tile([P, CH, PACK], BF16, name="d_bf%d" % c, align_bytes=64) for c in range(NCH)]
+        d_codes = keep.tile([P, J], U32, name="d_codes", align_bytes=64)
+        d_sc = keep.tile([P, J], U8, name="d_sc", align_bytes=64)
+
+        def weave(engine_copy, c, u):
+            engine_copy(d_bf[c][:, :, 2 * u : 2 * u + 2], d_pair[u][:, :, c * CH : (c + 1) * CH].rearrange("p e j -> p j e"))
+
+        def scalar_copy(out, in_):
+            nc.scalar.activation(out, in_, COPY)
+
+        for t in range(PACK - 1):
+            nc.vector.tensor_copy(tb_got[t][:], tb_sb[t][:].indirect(tb_list[:]))
+            nc.vector.tensor_tensor(d_pair[t // 2][:, t % 2, :], g_sb[t][:].indirect(g_list[:]), tb_got[t][:], MULT)
+            if t == 1:
+                for c in range(NCH):
+                    weave(scalar_copy, c, 0)
+        t = PACK - 1
+        nc.vector.tensor_copy(tb_got[t][:], tb_sb[t][:].indirect(tb_list[:]))
+
+        y_sc = keep.tile([P, J], U8, name="y_sc", align_bytes=64)
+        y_rows = out_0.rearrange("(p t) j -> p t j", t=PACK)
+        y_words = out_1[0].rearrange("p n t -> p (n t)")
+
+        def gather_last(c):
+            cols = slice(c * CH, (c + 1) * CH)
+            nc.vector.tensor_tensor(
+                d_pair[1][:, 1, cols], g_sb[t][:].indirect(g_list[:, c * LC : (c + 1) * LC]), tb_got[t][:, cols], MULT
+            )
+            weave(nc.vector.tensor_copy if c == NCH - 1 else scalar_copy, c, 1)
+
+        for c in range(NCH):
+            gather_last(c)
+        for c in range(NCH):
+            cols = slice(c * CH, (c + 1) * CH)
+            if c == NCH - 1:
+                nc.vector.tensor_copy(
+                    w_codes[:].rearrange("p t (c i) -> p c t i", i=4), w_raw[:].rearrange("p (c i t) -> p c t i", i=4, t=PACK)
+                )
+            nc.vector.quantize_mx(d_codes[:, cols].bitcast(E5M2), d_sc[:, cols], d_bf[c][:].rearrange("p j t -> p (j t)"))
+
+        half = J // 2
+        y_pair = [keep.tile([P, 2, J], F32, name="y_pair%d" % u) for u in range(2)]
+        y_bf = [keep.tile([P, half, PACK], BF16, name="y_bf%d" % h, align_bytes=64) for h in range(2)]
+        y_codes = [keep.tile([P, half], U32, name="y_codes%d" % h, align_bytes=64) for h in range(2)]
+
+        def weave_y(engine_copy, h, u):
+            engine_copy(y_bf[h][:, :, 2 * u : 2 * u + 2], y_pair[u][:, :, h * half : (h + 1) * half].rearrange("p e j -> p j e"))
+
+        for r in range(PACK):
+            acc = psum.tile([P, J], F32, name="acc%d" % r)
+            nc.tensor.matmul_mx(
+                acc[:], lhsT=w_codes[:, r, :].bitcast(E4M3), lhsT_scale=w_sc[:, r, :],
+                rhs=d_codes[:].bitcast(E5M2), rhs_scale=d_sc[:], start=True, stop=True,
+            )
+            plane = y_pair[r // 2][:, r % 2, :]
+            if r < PACK - 1:
+                nc.vector.tensor_tensor(plane, acc[:], rw_all[:], MULT)
+            else:
+                for h in range(2):
+                    cols = slice(h * half, (h + 1) * half)
+                    nc.vector.tensor_tensor(plane[:, cols], acc[:, cols], rw_all[:, cols], MULT)
+            nc.sync.dma_start(y_rows[:, r, :], plane)
+            if r == 1:
+                for h in range(2):
+                    weave_y(scalar_copy, h, 0)
+        for h in range(2):
+            weave_y(nc.vector.tensor_copy, h, 1)
+        for h in range(2):
+            cols = slice(h * half, (h + 1) * half)
+            nc.vector.quantize_mx(y_codes[h][:].bitcast(E4M3), y_sc[:, cols], y_bf[h][:].rearrange("p j t -> p (j t)"))
+            nc.sync.dma_start(y_words[:, h * half * PACK : (h + 1) * half * PACK].bitcast(I32), y_codes[h][:].bitcast(I32))
+        for q in range(4):
+            queue = nc.scalar if q % 2 else nc.sync
+            queue.dma_start(out_2[0, 4 * q : 4 * q + 4, :].bitcast(I32), y_sc[32 * q : 32 * q + 4, :].bitcast(I32))

@@ -37,27 +37,29 @@ def tile_moe_expert_head_gradients_by_table_pl_kernel(tc, g, tb, w_words, w_scal
         g_sb = [keep.tile([P, T], F32, name="g_sb%d" % t) for t in range(PACK)]
         tb_sb = [keep.tile([P, V], F32, name="tb_sb%d" % t) for t in range(PACK)]
 
-        nc.sync.dma_start(tb_list[:], offs2)
-        nc.sync.dma_start(tb_sb[0][:], tb_rows[:, 0, :])
-        nc.sync.dma_start(g_list[:], offs)
-        nc.sync.dma_start(g_sb[0][:], g_rows[:, 0, :])
-        for t in range(1, PACK):
-            nc.sync.dma_start(tb_sb[t][:], tb_rows[:, t, :])
-            nc.sync.dma_start(g_sb[t][:], g_rows[:, t, :])
-
-        w_raw = keep.tile([P, K], I32, name="w_raw")
-        w_codes = keep.tile([P, PACK, P], I32, name="w_codes", align_bytes=64)
         sc_raw = keep.tile([P, K], U8, name="sc_raw")
         w_sc = keep.tile([P, PACK, P], U8, name="w_sc", align_bytes=64)
-        rw_col = keep.tile([P, PACK], F32, name="rw_col")
-        nc.vector.memset(sc_raw[:].bitcast(I32), 0)
+        nc.gpsimd.memset(sc_raw[:].bitcast(I32), 0)
         for q in range(4):
             nc.scalar.dma_start(sc_raw[32 * q : 32 * q + 4, :].bitcast(I32), w_scales[0, 4 * q : 4 * q + 4, :].bitcast(I32))
-        nc.sync.dma_start(w_raw[:], w_words[0].rearrange("p n t -> p (n t)").bitcast(I32))
-        nc.sync.dma_start(rw_col[:], rw.rearrange("o (p c) -> p (o c)", c=PACK))
         nc.vector.tensor_copy(
             w_sc[:].rearrange("p t (c i) -> p c t i", i=16), sc_raw[:].rearrange("p (c i t) -> p c t i", i=16, t=PACK)
         )
+
+        nc.sync.dma_start(tb_list[:], offs2)
+        nc.sync.dma_start(tb_sb[0][:], tb_rows[:, 0, :])
+        nc.sync.dma_start(g_list[:], offs)
+        nc.sync.dma_start(tb_sb[1][:], tb_rows[:, 1, :])
+        for t in range(PACK):
+            nc.sync.dma_start(g_sb[t][:], g_rows[:, t, :])
+            if t + 2 < PACK:
+                nc.sync.dma_start(tb_sb[t + 2][:], tb_rows[:, t + 2, :])
+
+        w_raw = keep.tile([P, K], I32, name="w_raw")
+        w_codes = keep.tile([P, PACK, P], I32, name="w_codes", align_bytes=64)
+        rw_col = keep.tile([P, PACK], F32, name="rw_col")
+        nc.sync.dma_start(w_raw[:], w_words[0].rearrange("p n t -> p (n t)").bitcast(I32))
+        nc.sync.dma_start(rw_col[:], rw.rearrange("o (p c) -> p (o c)", c=PACK))
 
         ident = keep.tile([P, P], F32, name="ident")
         make_identity(nc, ident[:])
@@ -73,34 +75,26 @@ def tile_moe_expert_head_gradients_by_table_pl_kernel(tc, g, tb, w_words, w_scal
         d_codes = keep.tile([P, J], U32, name="d_codes", align_bytes=64)
         d_sc = keep.tile([P, J], U8, name="d_sc", align_bytes=64)
 
-        def weave(engine_copy, c, u):
-            engine_copy(d_bf[c][:, :, 2 * u : 2 * u + 2], d_pair[u][:, :, c * CH : (c + 1) * CH].rearrange("p e j -> p j e"))
+        def weave_d(c, u):
+            nc.scalar.copy(d_bf[c][:, :, 2 * u : 2 * u + 2], d_pair[u][:, :, c * CH : (c + 1) * CH].rearrange("p e j -> p j e"))
 
-        def scalar_copy(out, in_):
-            nc.scalar.activation(out, in_, COPY)
-
-        for t in range(PACK - 1):
+        def gather_tb(t):
             nc.vector.tensor_copy(tb_got[t][:], tb_sb[t][:].indirect(tb_list[:]))
+
+        gather_tb(0)
+        for t in range(PACK - 1):
+            gather_tb(t + 1)
             nc.vector.tensor_tensor(d_pair[t // 2][:, t % 2, :], g_sb[t][:].indirect(g_list[:]), tb_got[t][:], MULT)
             if t == 1:
                 for c in range(NCH):
-                    weave(scalar_copy, c, 0)
-        t = PACK - 1
-        nc.vector.tensor_copy(tb_got[t][:], tb_sb[t][:].indirect(tb_list[:]))
-
-        y_sc = keep.tile([P, J], U8, name="y_sc", align_bytes=64)
-        y_rows = out_0.rearrange("(p t) j -> p t j", t=PACK)
-        y_words = out_1[0].rearrange("p n t -> p (n t)")
-
-        def gather_last(c):
+                    weave_d(c, 0)
+        last = PACK - 1
+        for c in range(NCH):
             cols = slice(c * CH, (c + 1) * CH)
             nc.vector.tensor_tensor(
-                d_pair[1][:, 1, cols], g_sb[t][:].indirect(g_list[:, c * LC : (c + 1) * LC]), tb_got[t][:, cols], MULT
+                d_pair[1][:, 1, cols], g_sb[last][:].indirect(g_list[:, c * LC : (c + 1) * LC]), tb_got[last][:, cols], MULT
             )
-            weave(nc.vector.tensor_copy if c == NCH - 1 else scalar_copy, c, 1)
-
-        for c in range(NCH):
-            gather_last(c)
+            weave_d(c, 1)
         for c in range(NCH):
             cols = slice(c * CH, (c + 1) * CH)
             if c == NCH - 1:
@@ -110,12 +104,15 @@ def tile_moe_expert_head_gradients_by_table_pl_kernel(tc, g, tb, w_words, w_scal
             nc.vector.quantize_mx(d_codes[:, cols].bitcast(E5M2), d_sc[:, cols], d_bf[c][:].rearrange("p j t -> p (j t)"))
 
         half = J // 2
-        y_pair = [keep.tile([P, 2, J], F32, name="y_pair%d" % u) for u in range(2)]
+        y_sc = keep.tile([P, J], U8, name="y_sc", align_bytes=64)
+        y_rows = out_0.rearrange("(p t) j -> p t j", t=PACK)
+        y_words = out_1[0].rearrange("p n t -> p (n t)")
+        y_f = keep.tile([P, PACK, J], F32, name="y_f")
         y_bf = [keep.tile([P, half, PACK], BF16, name="y_bf%d" % h, align_bytes=64) for h in range(2)]
         y_codes = [keep.tile([P, half], U32, name="y_codes%d" % h, align_bytes=64) for h in range(2)]
 
-        def weave_y(engine_copy, h, u):
-            engine_copy(y_bf[h][:, :, 2 * u : 2 * u + 2], y_pair[u][:, :, h * half : (h + 1) * half].rearrange("p e j -> p j e"))
+        def weave_y(u):
+            nc.scalar.copy(y_bf[0][:, :, 2 * u : 2 * u + 2], y_f[:, 2 * u : 2 * u + 2, 0:half].rearrange("p e j -> p j e"))
 
         for r in range(PACK):
             acc = psum.tile([P, J], F32, name="acc%d" % r)
@@ -123,19 +120,20 @@ def tile_moe_expert_head_gradients_by_table_pl_kernel(tc, g, tb, w_words, w_scal
                 acc[:], lhsT=w_codes[:, r, :].bitcast(E4M3), lhsT_scale=w_sc[:, r, :],
                 rhs=d_codes[:].bitcast(E5M2), rhs_scale=d_sc[:], start=True, stop=True,
             )
-            plane = y_pair[r // 2][:, r % 2, :]
             if r < PACK - 1:
-                nc.vector.tensor_tensor(plane, acc[:], rw_all[:], MULT)
+                nc.vector.tensor_tensor(y_f[:, r, :], acc[:], rw_all[:], MULT)
             else:
                 for h in range(2):
                     cols = slice(h * half, (h + 1) * half)
-                    nc.vector.tensor_tensor(plane[:, cols], acc[:, cols], rw_all[:, cols], MULT)
-            nc.sync.dma_start(y_rows[:, r, :], plane)
+                    nc.vector.tensor_tensor(y_f[:, r, cols], acc[:, cols], rw_all[:, cols], MULT)
+                    if h == 0:
+                        weave_y(1)
+            nc.sync.dma_start(y_rows[:, r, :], y_f[:, r, :])
             if r == 1:
-                for h in range(2):
-                    weave_y(scalar_copy, h, 0)
-        for h in range(2):
-            weave_y(nc.vector.tensor_copy, h, 1)
+                weave_y(0)
+        nc.vector.tensor_copy(
+            y_bf[1][:].rearrange("p (c i) t -> p c t i", i=4), y_f[:, :, half:J].rearrange("p t (c i) -> p c t i", i=4)
+        )
         for h in range(2):
             cols = slice(h * half, (h + 1) * half)
             nc.vector.quantize_mx(y_codes[h][:].bitcast(E4M3), y_sc[:, cols], y_bf[h][:].rearrange("p j t -> p (j t)"))

@@ -38,13 +38,9 @@ def tile_moe_expert_head_gradients_by_table_pl_kernel(tc, g, tb, w_words, w_scal
         tb_sb = [keep.tile([P, V], F32, name="tb_sb%d" % t) for t in range(PACK)]
 
         sc_raw = keep.tile([P, K], U8, name="sc_raw")
-        w_sc = keep.tile([P, PACK, P], U8, name="w_sc", align_bytes=64)
+        sc_first = keep.tile([P, P], U8, name="sc_first", align_bytes=64)
         nc.gpsimd.memset(sc_raw[:].bitcast(I32), 0)
-        for q in range(4):
-            nc.scalar.dma_start(sc_raw[32 * q : 32 * q + 4, :].bitcast(I32), w_scales[0, 4 * q : 4 * q + 4, :].bitcast(I32))
-        nc.vector.tensor_copy(
-            w_sc[:].rearrange("p t (c i) -> p c t i", i=16), sc_raw[:].rearrange("p (c i t) -> p c t i", i=16, t=PACK)
-        )
+        rw_col = keep.tile([P, PACK], F32, name="rw_col")
 
         nc.sync.dma_start(tb_list[:], offs2)
         nc.sync.dma_start(tb_sb[0][:], tb_rows[:, 0, :])
@@ -54,12 +50,18 @@ def tile_moe_expert_head_gradients_by_table_pl_kernel(tc, g, tb, w_words, w_scal
             nc.sync.dma_start(g_sb[t][:], g_rows[:, t, :])
             if t + 2 < PACK:
                 nc.sync.dma_start(tb_sb[t + 2][:], tb_rows[:, t + 2, :])
+            if t == 0:
+                nc.sync.dma_start(rw_col[:], rw.rearrange("o (p c) -> p (o c)", c=PACK))
+            if t == 1:
+                for q in range(4):
+                    nc.sync.dma_start(
+                        sc_raw[32 * q : 32 * q + 4, :].bitcast(I32), w_scales[0, 4 * q : 4 * q + 4, :].bitcast(I32)
+                    )
 
         w_raw = keep.tile([P, K], I32, name="w_raw")
-        w_codes = keep.tile([P, PACK, P], I32, name="w_codes", align_bytes=64)
-        rw_col = keep.tile([P, PACK], F32, name="rw_col")
+        w_first = keep.tile([P, P], I32, name="w_first", align_bytes=64)
         nc.sync.dma_start(w_raw[:], w_words[0].rearrange("p n t -> p (n t)").bitcast(I32))
-        nc.sync.dma_start(rw_col[:], rw.rearrange("o (p c) -> p (o c)", c=PACK))
+        nc.vector.tensor_copy(sc_first[:], sc_raw[:, 0:K:PACK])
 
         ident = keep.tile([P, P], F32, name="ident")
         make_identity(nc, ident[:])
@@ -70,7 +72,7 @@ def tile_moe_expert_head_gradients_by_table_pl_kernel(tc, g, tb, w_words, w_scal
         nc.scalar.copy(rw_all[:].rearrange("p (n c) -> p n c", c=PACK), rw_bank[:].rearrange("p c n -> p n c"))
 
         tb_got = [keep.tile([P, J], F32, name="tb_got%d" % t) for t in range(PACK)]
-        d_pair = [keep.tile([P, 2, J], F32, name="d_pair%d" % u) for u in range(2)]
+        d_pair = [keep.tile([P, 2, J], F32, name="d_pair%d" % u, align_bytes=64) for u in range(2)]
         d_bf = [keep.tile([P, CH, PACK], BF16, name="d_bf%d" % c, align_bytes=64) for c in range(NCH)]
         d_codes = keep.tile([P, J], U32, name="d_codes", align_bytes=64)
         d_sc = keep.tile([P, J], U8, name="d_sc", align_bytes=64)
@@ -97,11 +99,21 @@ def tile_moe_expert_head_gradients_by_table_pl_kernel(tc, g, tb, w_words, w_scal
             weave_d(c, 1)
         for c in range(NCH):
             cols = slice(c * CH, (c + 1) * CH)
-            if c == NCH - 1:
-                nc.vector.tensor_copy(
-                    w_codes[:].rearrange("p t (c i) -> p c t i", i=4), w_raw[:].rearrange("p (c i t) -> p c t i", i=4, t=PACK)
-                )
+            if c == 2:
+                nc.vector.tensor_copy(w_first[:], w_raw[:, 0:K:PACK])
             nc.vector.quantize_mx(d_codes[:, cols].bitcast(E5M2), d_sc[:, cols], d_bf[c][:].rearrange("p j t -> p (j t)"))
+        sc_rest = keep.tile([P, PACK - 1, P], U8, name="sc_rest", tag="d_pair1", align_bytes=64)
+        w_rest = keep.tile([P, PACK - 1, P], I32, name="w_rest", tag="d_bf3", align_bytes=64)
+        nc.vector.tensor_copy(
+            sc_rest[:].rearrange("p t (c i) -> p c t i", i=16),
+            sc_raw[:].rearrange("p (c i t) -> p c t i", i=16, t=PACK)[:, :, 1:PACK, :],
+        )
+        nc.vector.tensor_copy(
+            w_rest[:].rearrange("p t (c i) -> p c t i", i=4),
+            w_raw[:].rearrange("p (c i t) -> p c t i", i=4, t=PACK)[:, :, 1:PACK, :],
+        )
+        w_codes = [w_first[:]] + [w_rest[:, r, :] for r in range(PACK - 1)]
+        w_sc = [sc_first[:]] + [sc_rest[:, r, :] for r in range(PACK - 1)]
 
         half = J // 2
         y_sc = keep.tile([P, J], U8, name="y_sc", align_bytes=64)
@@ -111,33 +123,44 @@ def tile_moe_expert_head_gradients_by_table_pl_kernel(tc, g, tb, w_words, w_scal
         y_bf = [keep.tile([P, half, PACK], BF16, name="y_bf%d" % h, align_bytes=64) for h in range(2)]
         y_codes = [keep.tile([P, half], U32, name="y_codes%d" % h, align_bytes=64) for h in range(2)]
 
-        def weave_y(u):
-            nc.scalar.copy(y_bf[0][:, :, 2 * u : 2 * u + 2], y_f[:, 2 * u : 2 * u + 2, 0:half].rearrange("p e j -> p j e"))
+        def weave_y(engine_copy, u, lo, hi):
+            h = lo // half
+            engine_copy(
+                y_bf[h][:, lo - h * half : hi - h * half, 2 * u : 2 * u + 2],
+                y_f[:, 2 * u : 2 * u + 2, lo:hi].rearrange("p e j -> p j e"),
+            )
 
         for r in range(PACK):
             acc = psum.tile([P, J], F32, name="acc%d" % r)
             nc.tensor.matmul_mx(
-                acc[:], lhsT=w_codes[:, r, :].bitcast(E4M3), lhsT_scale=w_sc[:, r, :],
+                acc[:], lhsT=w_codes[r].bitcast(E4M3), lhsT_scale=w_sc[r],
                 rhs=d_codes[:].bitcast(E5M2), rhs_scale=d_sc[:], start=True, stop=True,
             )
             if r < PACK - 1:
                 nc.vector.tensor_tensor(y_f[:, r, :], acc[:], rw_all[:], MULT)
             else:
-                for h in range(2):
-                    cols = slice(h * half, (h + 1) * half)
-                    nc.vector.tensor_tensor(y_f[:, r, cols], acc[:, cols], rw_all[:, cols], MULT)
-                    if h == 0:
-                        weave_y(1)
+                for lo, hi in ((0, half), (3 * CH, J), (half, 3 * CH)):
+                    nc.vector.tensor_tensor(y_f[:, r, lo:hi], acc[:, lo:hi], rw_all[:, lo:hi], MULT)
+                weave_y(nc.scalar.copy, 1, 0, CH)
+                weave_y(nc.scalar.copy, 1, CH, half)
             nc.sync.dma_start(y_rows[:, r, :], y_f[:, r, :])
             if r == 1:
-                weave_y(0)
+                weave_y(nc.scalar.copy, 0, 0, half)
+                weave_y(nc.scalar.copy, 0, half, half + CH)
         nc.vector.tensor_copy(
-            y_bf[1][:].rearrange("p (c i) t -> p c t i", i=4), y_f[:, :, half:J].rearrange("p t (c i) -> p c t i", i=4)
+            y_bf[1][:, CH:half, :].rearrange("p (c i) t -> p c t i", i=4),
+            y_f[:, :, half + CH : J].rearrange("p t (c i) -> p c t i", i=4),
         )
-        for h in range(2):
-            cols = slice(h * half, (h + 1) * half)
-            nc.vector.quantize_mx(y_codes[h][:].bitcast(E4M3), y_sc[:, cols], y_bf[h][:].rearrange("p j t -> p (j t)"))
-            nc.sync.dma_start(y_words[:, h * half * PACK : (h + 1) * half * PACK].bitcast(I32), y_codes[h][:].bitcast(I32))
+        weave_y(nc.vector.tensor_copy, 1, half, half + CH)
+        for h, lo, hi in ((1, CH, half), (0, 0, CH), (1, 0, CH), (0, CH, half)):
+            nc.vector.quantize_mx(
+                y_codes[h][:, lo:hi].bitcast(E4M3),
+                y_sc[:, h * half + lo : h * half + hi],
+                y_bf[h][:, lo:hi, :].rearrange("p j t -> p (j t)"),
+            )
+            nc.sync.dma_start(
+                y_words[:, (h * half + lo) * PACK : (h * half + hi) * PACK].bitcast(I32), y_codes[h][:, lo:hi].bitcast(I32)
+            )
         for q in range(4):
-            queue = nc.scalar if q % 2 else nc.sync
+            queue = nc.sync if q == 3 else nc.scalar
             queue.dma_start(out_2[0, 4 * q : 4 * q + 4, :].bitcast(I32), y_sc[32 * q : 32 * q + 4, :].bitcast(I32))

@@ -42,8 +42,8 @@ def tile_moe_expert_head_gradients_by_table_pl_kernel(tc, g, tb, w_words, w_scal
         nc.gpsimd.memset(sc_raw[:].bitcast(I32), 0)
         rw_col = keep.tile([P, PACK], F32, name="rw_col")
 
-        nc.sync.dma_start(tb_list[:], offs2)
         nc.sync.dma_start(tb_sb[0][:], tb_rows[:, 0, :])
+        nc.sync.dma_start(tb_list[:], offs2)
         nc.sync.dma_start(g_list[:], offs)
         nc.sync.dma_start(tb_sb[1][:], tb_rows[:, 1, :])
         for t in range(PACK):
@@ -77,8 +77,8 @@ def tile_moe_expert_head_gradients_by_table_pl_kernel(tc, g, tb, w_words, w_scal
         d_codes = keep.tile([P, J], U32, name="d_codes", align_bytes=64)
         d_sc = keep.tile([P, J], U8, name="d_sc", align_bytes=64)
 
-        def weave_d(c, u):
-            nc.scalar.copy(d_bf[c][:, :, 2 * u : 2 * u + 2], d_pair[u][:, :, c * CH : (c + 1) * CH].rearrange("p e j -> p j e"))
+        def weave_d(engine_copy, c, u):
+            engine_copy(d_bf[c][:, :, 2 * u : 2 * u + 2], d_pair[u][:, :, c * CH : (c + 1) * CH].rearrange("p e j -> p j e"))
 
         def gather_tb(t):
             nc.vector.tensor_copy(tb_got[t][:], tb_sb[t][:].indirect(tb_list[:]))
@@ -89,16 +89,19 @@ def tile_moe_expert_head_gradients_by_table_pl_kernel(tc, g, tb, w_words, w_scal
             nc.vector.tensor_tensor(d_pair[t // 2][:, t % 2, :], g_sb[t][:].indirect(g_list[:]), tb_got[t][:], MULT)
             if t == 1:
                 for c in range(NCH):
-                    weave_d(c, 0)
+                    weave_d(nc.scalar.copy, c, 0)
         last = PACK - 1
         for c in range(NCH):
             cols = slice(c * CH, (c + 1) * CH)
             nc.vector.tensor_tensor(
                 d_pair[1][:, 1, cols], g_sb[last][:].indirect(g_list[:, c * LC : (c + 1) * LC]), tb_got[last][:, cols], MULT
             )
-            weave_d(c, 1)
+            if c < NCH - 1:
+                weave_d(nc.scalar.copy, c, 1)
         for c in range(NCH):
             cols = slice(c * CH, (c + 1) * CH)
+            if c == 1:
+                weave_d(nc.vector.tensor_copy, NCH - 1, 1)
             if c == 2:
                 nc.vector.tensor_copy(w_first[:], w_raw[:, 0:K:PACK])
             nc.vector.quantize_mx(d_codes[:, cols].bitcast(E5M2), d_sc[:, cols], d_bf[c][:].rearrange("p j t -> p (j t)"))
@@ -152,15 +155,18 @@ def tile_moe_expert_head_gradients_by_table_pl_kernel(tc, g, tb, w_words, w_scal
             y_f[:, :, half + CH : J].rearrange("p t (c i) -> p c t i", i=4),
         )
         weave_y(nc.vector.tensor_copy, 1, half, half + CH)
-        for h, lo, hi in ((1, CH, half), (0, 0, CH), (1, 0, CH), (0, CH, half)):
+        for h, lo, hi, first in ((1, CH, half, None), (0, 0, CH, None), (1, 0, CH, 0), (0, CH, half, 0)):
             nc.vector.quantize_mx(
                 y_codes[h][:, lo:hi].bitcast(E4M3),
                 y_sc[:, h * half + lo : h * half + hi],
                 y_bf[h][:, lo:hi, :].rearrange("p j t -> p (j t)"),
             )
-            nc.sync.dma_start(
-                y_words[:, (h * half + lo) * PACK : (h * half + hi) * PACK].bitcast(I32), y_codes[h][:, lo:hi].bitcast(I32)
-            )
+            if first is not None:
+                end = half
+                nc.sync.dma_start(
+                    y_words[:, (h * half + first) * PACK : (h * half + end) * PACK].bitcast(I32),
+                    y_codes[h][:, first:end].bitcast(I32),
+                )
         for q in range(4):
             queue = nc.sync if q == 3 else nc.scalar
             queue.dma_start(out_2[0, 4 * q : 4 * q + 4, :].bitcast(I32), y_sc[32 * q : 32 * q + 4, :].bitcast(I32))

from contextlib import ExitStack

import concourse.mybir as mybir
from concourse.masks import make_identity

N, K, T, J, V = 512, 512, 1024, 512, 1024
FLOPS = 2 * N * K * J

F32 = mybir.dt.float32
BF16 = mybir.dt.bfloat16
I32 = mybir.dt.int32
U32 = mybir.dt.uint32
U16 = mybir.dt.uint16
U8 = mybir.dt.uint8
E4M3 = mybir.dt.float8_e4m3fn_x4
E5M2 = mybir.dt.float8_e5m2_x4
COPY = mybir.ActivationFunctionType.Copy
MULT = mybir.AluOpType.mult

P = 128
PACK = 4
CH = 128
NCH = J // CH
LC = CH // 16


def tile_moe_expert_head_gradients_by_table_pl_kernel(tc, g, tb, w_words, w_scales, rw, offs, offs2, out_0, out_1, out_2):
    nc = tc.nc
    with ExitStack() as ctx:
        keep = ctx.enter_context(tc.tile_pool(name="keep", bufs=1))
        psum = ctx.enter_context(tc.psum_pool(name="psum", bufs=1))

        g_list = keep.tile([P, J // 16], U16, name="g_list")
        tb_list = keep.tile([P, J // 16], U16, name="tb_list")
        g_rows = g.rearrange("(p t) c -> p t c", t=PACK)
        tb_rows = tb.rearrange("(p t) c -> p t c", t=PACK)
        g_sb = [keep.tile([P, T], F32, name="g_sb%d" % t) for t in range(PACK)]
        tb_sb = [keep.tile([P, V], F32, name="tb_sb%d" % t) for t in range(PACK)]

        sc_raw = keep.tile([P, K], U8, name="sc_raw")
        sc_first = keep.tile([P, P], U8, name="sc_first", align_bytes=64)
        nc.gpsimd.memset(sc_raw[:].bitcast(I32), 0)
        rw_col = keep.tile([P, PACK], F32, name="rw_col")

        nc.sync.dma_start(tb_sb[0][:], tb_rows[:, 0, :])
        nc.sync.dma_start(tb_list[:], offs2)
        nc.sync.dma_start(g_list[:], offs)
        nc.sync.dma_start(tb_sb[1][:], tb_rows[:, 1, :])
        for t in range(PACK):
            nc.sync.dma_start(g_sb[t][:], g_rows[:, t, :])
            if t + 2 < PACK:
                nc.sync.dma_start(tb_sb[t + 2][:], tb_rows[:, t + 2, :])
            if t == 0:
                nc.sync.dma_start(rw_col[:], rw.rearrange("o (p c) -> p (o c)", c=PACK))
            if t == 1:
                for q in range(4):
                    nc.sync.dma_start(
                        sc_raw[32 * q : 32 * q + 4, :].bitcast(I32), w_scales[0, 4 * q : 4 * q + 4, :].bitcast(I32)
                    )

        w_raw = keep.tile([P, K], I32, name="w_raw")
        w_first = keep.tile([P, P], I32, name="w_first", align_bytes=64)
        nc.sync.dma_start(w_raw[:], w_words[0].rearrange("p n t -> p (n t)").bitcast(I32))
        nc.vector.tensor_copy(sc_first[:], sc_raw[:, 0:K:PACK])

        ident = keep.tile([P, P], F32, name="ident")
        make_identity(nc, ident[:])
        rw_bank = psum.tile([P, PACK, P], F32, name="rw_bank")
        for c in range(PACK):
            nc.tensor.transpose(rw_bank[:, c, :], rw_col[:, c : c + 1].to_broadcast([P, P]), ident[:])
        rw_all = keep.tile([P, J], F32, name="rw_all")
        nc.scalar.copy(rw_all[:].rearrange("p (n c) -> p n c", c=PACK), rw_bank[:].rearrange("p c n -> p n c"))

        tb_got = [keep.tile([P, J], F32, name="tb_got%d" % t) for t in range(PACK)]
        d_pair = [keep.tile([P, 2, J], F32, name="d_pair%d" % u, align_bytes=64) for u in range(2)]
        d_bf = [keep.tile([P, CH, PACK], BF16, name="d_bf%d" % c, align_bytes=64) for c in range(NCH)]
        d_codes = keep.tile([P, J], U32, name="d_codes", align_bytes=64)
        d_sc = keep.tile([P, J], U8, name="d_sc", align_bytes=64)

        def weave_d(engine_copy, c, u):
            engine_copy(d_bf[c][:, :, 2 * u : 2 * u + 2], d_pair[u][:, :, c * CH : (c + 1) * CH].rearrange("p e j -> p j e"))

        def gather_tb(t):
            nc.vector.tensor_copy(tb_got[t][:], tb_sb[t][:].indirect(tb_list[:]))

        gather_tb(0)
        for t in range(PACK - 1):
            gather_tb(t + 1)
            nc.vector.tensor_tensor(d_pair[t // 2][:, t % 2, :], g_sb[t][:].indirect(g_list[:]), tb_got[t][:], MULT)
            if t == 1:
                for c in range(NCH):
                    weave_d(nc.scalar.copy, c, 0)
        last = PACK - 1
        for c in range(NCH):
            cols = slice(c * CH, (c + 1) * CH)
            nc.vector.tensor_tensor(
                d_pair[1][:, 1, cols], g_sb[last][:].indirect(g_list[:, c * LC : (c + 1) * LC]), tb_got[last][:, cols], MULT
            )
            if c < NCH - 1:
                weave_d(nc.scalar.copy, c, 1)
        for c in range(NCH):
            cols = slice(c * CH, (c + 1) * CH)
            if c == 1:
                weave_d(nc.vector.tensor_copy, NCH - 1, 1)
            if c == 2:
                nc.vector.tensor_copy(w_first[:], w_raw[:, 0:K:PACK])
            nc.vector.quantize_mx(d_codes[:, cols].bitcast(E5M2), d_sc[:, cols], d_bf[c][:].rearrange("p j t -> p (j t)"))
        sc_rest = keep.tile([P, PACK - 1, P], U8, name="sc_rest", tag="d_pair1", align_bytes=64)
        w_rest = keep.tile([P, PACK - 1, P], I32, name="w_rest", tag="d_bf3", align_bytes=64)
        nc.vector.tensor_copy(
            sc_rest[:].rearrange("p t (c i) -> p c t i", i=16),
            sc_raw[:].rearrange("p (c i t) -> p c t i", i=16, t=PACK)[:, :, 1:PACK, :],
        )
        nc.vector.tensor_copy(
            w_rest[:].rearrange("p t (c i) -> p c t i", i=4),
            w_raw[:].rearrange("p (c i t) -> p c t i", i=4, t=PACK)[:, :, 1:PACK, :],
        )
        w_codes = [w_first[:]] + [w_rest[:, r, :] for r in range(PACK - 1)]
        w_sc = [sc_first[:]] + [sc_rest[:, r, :] for r in range(PACK - 1)]

        half = J // 2
        y_sc = keep.tile([P, J], U8, name="y_sc", align_bytes=64)
        y_rows = out_0.rearrange("(p t) j -> p t j", t=PACK)
        y_words = out_1[0].rearrange("p n t -> p (n t)")
        y_f = keep.tile([P, PACK, J], F32, name="y_f")
        y_bf = [keep.tile([P, half, PACK], BF16, name="y_bf%d" % h, align_bytes=64) for h in range(2)]
        y_codes = [keep.tile([P, half], U32, name="y_codes%d" % h, align_bytes=64) for h in range(2)]

        def weave_y(engine_copy, u, lo, hi):
            h = lo // half
            engine_copy(
                y_bf[h][:, lo - h * half : hi - h * half, 2 * u : 2 * u + 2],
                y_f[:, 2 * u : 2 * u + 2, lo:hi].rearrange("p e j -> p j e"),
            )

        for r in range(PACK):
            acc = psum.tile([P, J], F32, name="acc%d" % r)
            nc.tensor.matmul_mx(
                acc[:], lhsT=w_codes[r].bitcast(E4M3), lhsT_scale=w_sc[r],
                rhs=d_codes[:].bitcast(E5M2), rhs_scale=d_sc[:], start=True, stop=True,
            )
            if r < PACK - 1:
                nc.vector.tensor_tensor(y_f[:, r, :], acc[:], rw_all[:], MULT)
            else:
                for lo, hi in ((0, half), (3 * CH, J), (half, 3 * CH)):
                    nc.vector.tensor_tensor(y_f[:, r, lo:hi], acc[:, lo:hi], rw_all[:, lo:hi], MULT)
                weave_y(nc.scalar.copy, 1, 0, CH)
                weave_y(nc.scalar.copy, 1, CH, half)
            nc.sync.dma_start(y_rows[:, r, :], y_f[:, r, :])
            if r == 1:
                weave_y(nc.scalar.copy, 0, 0, half)
                weave_y(nc.scalar.copy, 0, half, half + CH)
        nc.vector.tensor_copy(
            y_bf[1][:, CH:half, :].rearrange("p (c i) t -> p c t i", i=4),
            y_f[:, :, half + CH : J].rearrange("p t (c i) -> p c t i", i=4),
        )
        weave_y(nc.vector.tensor_copy, 1, half, half + CH)
        for h, lo, hi, first in ((1, CH, half, None), (0, 0, CH, None), (1, 0, CH, 0), (0, CH, half, 0)):
            nc.vector.quantize_mx(
                y_codes[h][:, lo:hi].bitcast(E4M3),
                y_sc[:, h * half + lo : h * half + hi],
                y_bf[h][:, lo:hi, :].rearrange("p j t -> p (j t)"),
            )
            if first is not None:
                end = half
                nc.sync.dma_start(
                    y_words[:, (h * half + first) * PACK : (h * half + end) * PACK].bitcast(I32),
                    y_codes[h][:, first:end].bitcast(I32),
                )
        for q in range(4):
            queue = nc.sync if q == 3 else nc.scalar
            queue.dma_start(out_2[0, 4 * q : 4 * q + 4, :].bitcast(I32), y_sc[32 * q : 32 * q + 4, :].bitcast(I32))
